import numpy as np
import ml_dtypes


def mxq(x, axis, fmt="e4m3"):
    dtype, down = {"e4m3": (ml_dtypes.float8_e4m3fn, 7), "e5m2": (ml_dtypes.float8_e5m2, 14)}[fmt]
    v = np.moveaxis(np.asarray(x, np.float32).astype(ml_dtypes.bfloat16).astype(np.float64), axis, -1)
    blocks = v.reshape(v.shape[:-1] + (-1, 32))
    amax = np.abs(blocks).max(-1, keepdims=True)
    byte = np.maximum(np.where(amax > 0, np.frexp(amax)[1] - 1 + 127, 0) - down, 1)
    scale = np.exp2(byte - 127.0)
    codes = (blocks / scale).astype(np.float32).astype(dtype).astype(np.float64)
    return np.moveaxis((codes * scale).reshape(v.shape), -1, axis)


WIDE = False


def mx_kscale(k):
    if not WIDE:
        return np.ones(k)
    levels = np.array([10, -10, 5, -5, 0])
    if k % 512:
        return np.exp2(np.random.permutation(np.resize(levels, k // 32))).repeat(32)
    a = np.empty((k // 512, 16))
    for p in range(k // 512):
        a[p, :8] = np.random.permutation(np.resize(levels, 8))
        for g in range(8):
            far = levels[np.abs(levels - a[p, g]) >= 10]
            a[p, g + 8] = far[np.random.randint(len(far))]
    return np.exp2(a.ravel()).repeat(32)


def f64(x):
    return np.asarray(x).astype(np.float64)


def striped(idx):
    return np.tile(idx.reshape(-1, 16).T, (8, 1)).astype(np.uint16)


def unstriped(offs):
    return offs[:16].T.reshape(-1).astype(np.int64)


E2M1 = np.array([0.0, 0.5, 1.0, 1.5, 2.0, 3.0, 4.0, 6.0, -0.0, -0.5, -1.0, -1.5, -2.0, -3.0, -4.0, -6.0])


def pack_weight(w, fmt):
    k, n = w.shape
    w = f64(np.asarray(w, np.float32).astype(ml_dtypes.bfloat16)).reshape(k // 32, 32, n)
    amax = np.abs(w).max(1)
    if fmt == "e4m3":
        byte = np.frexp(amax)[1] - 1 + 127 - 7
    else:
        mant, ex = np.frexp(amax / 6.0)
        byte = np.where(mant > 0.5, ex, ex - 1) + 127
    byte = np.clip(np.where(amax > 0, byte, 1), 1, 254)
    scaled = (w * np.exp2(127.0 - byte)[:, None, :]).reshape(k, n).astype(np.float32)
    by_word = np.ascontiguousarray(scaled.reshape(k // 512, 128, 4, n).transpose(0, 1, 3, 2))
    if fmt == "e4m3":
        words = by_word.astype(ml_dtypes.float8_e4m3fn).view(np.uint8)
    else:
        c = by_word.astype(ml_dtypes.float4_e2m1fn).view(np.uint8) & 0xF
        words = (c[..., 0::2] | (c[..., 1::2] << 4)).reshape(k // 512, 128, 2 * n)
    return np.ascontiguousarray(words), np.ascontiguousarray(byte.astype(np.uint8).reshape(k // 512, 16, n))


def unpack_weight(words, scales, fmt):
    g, _, n = scales.shape
    words = np.ascontiguousarray(words).reshape(g, 128, n, -1)
    if fmt == "e4m3":
        vals = words.view(ml_dtypes.float8_e4m3fn).astype(np.float64)
    else:
        nib = np.empty((g, 128, n, 4), np.uint8)
        nib[..., 0::2] = words & 0xF
        nib[..., 1::2] = words >> 4
        vals = E2M1[nib]
    vals = vals * np.repeat(np.exp2(scales.astype(np.float64) - 127.0), 8, axis=1)[..., None]
    return vals.transpose(0, 1, 3, 2).reshape(g * 512, n)


def gelu(v):
    return 0.5 * v * (1.0 + np.tanh(np.sqrt(2.0 / np.pi) * (v + 0.044715 * v**3)))


def bf(x):
    return np.asarray(x, np.float32).astype(ml_dtypes.bfloat16)


def planes(Y):
    n, m = Y.shape
    b = f64(bf(Y)).reshape(n // 32, 32, m)
    amax = np.abs(b).max(1)
    byte = np.clip(np.where(amax > 0, np.frexp(amax)[1] - 1 + 127 - 7, 1), 1, 254)
    codes = (b * np.exp2(127.0 - byte)[:, None, :]).reshape(n, m).astype(np.float32).astype(ml_dtypes.float8_e4m3fn).view(np.uint8)
    words = codes.reshape(n // 512, 128, 4, m).transpose(0, 1, 3, 2)
    return np.ascontiguousarray(words), np.ascontiguousarray(byte.astype(np.uint8).reshape(n // 512, 16, m))


K, T, S, H, T2, P, N = 1024, 4096, 1024, 1024, 2048, 1024, 384

def setup_inputs():
    n = np.random.standard_normal
    s = mx_kscale(K)[:, None]
    u = mx_kscale(H)[:, None]
    d = {}
    d["tab_words"], d["tab_scales"] = pack_weight(n((K, T)) * s, "e4m3")
    d["offs"] = striped(np.random.permutation(T)[:S])
    d["offs2"] = striped(np.random.permutation(T2)[:S])
    d["offs3"] = striped(np.random.permutation(T2)[:P])
    d["w1"] = (n((K, H)) / K**0.5 / s).astype(np.float32)
    d["depth"] = np.random.uniform(1.8, 2.8, H).astype(np.float32)
    d["gain"] = (np.random.uniform(0.8, 1.8, H) * u[:, 0]).astype(np.float32)
    d["wgs"] = np.exp(0.3 * n((128, S))).astype(np.float32)
    d["page0"] = (n((H, T2)) * u).astype(np.float32)
    d["sc"] = np.exp(0.4 * n(H)).astype(np.float32)
    d["w4_words"], d["w4_scales"] = pack_weight(n((H, N)) / H**0.5 / u, "e2m1")
    d["w5"] = (n((H, N)) / H**0.5 / u).astype(np.float32)
    return d

def reference(tab_words, tab_scales, offs, offs2, offs3, w1, depth, gain, wgs, page0, sc, w4_words, w4_scales, w5):
    v = unpack_weight(tab_words, tab_scales, "e4m3")[:, unstriped(offs)]
    phase = f64(depth)[:, None] * np.tanh(mxq(f64(w1), 0, "e4m3").T @ v)
    h = f64(gain)[:, None] * np.cos(phase)
    page = f64(page0).copy()
    page[:, unstriped(offs2)] = np.tile(f64(wgs), (H // 128, 1)) * h
    x = f64(sc)[:, None] * page[:, unstriped(offs3)]
    w4 = unpack_weight(w4_words, w4_scales, "e2m1")
    y = w4.T @ mxq(x, 0, "e4m3") + mxq(f64(w5), 0, "e4m3").T @ mxq(h, 0, "e4m3")
    words, scales = planes(page)
    return y, page, words, scales

@@ -1,0 +1,335 @@
+from contextlib import ExitStack
+
+import concourse.mybir as mybir
+
+K, T, S, H, T2, NP, N = 1024, 4096, 1024, 1024, 2048, 1024, 384
+FLOPS = 2 * K * H * S + 2 * 2 * H * N * NP
+
+F32 = mybir.dt.float32
+BF16 = mybir.dt.bfloat16
+I32 = mybir.dt.int32
+U32 = mybir.dt.uint32
+U16 = mybir.dt.uint16
+U8 = mybir.dt.uint8
+FP8X4 = mybir.dt.float8_e4m3fn_x4
+FP4X4 = mybir.dt.float4_e2m1fn_x4
+ACT = mybir.ActivationFunctionType
+ALU = mybir.AluOpType
+
+P = 128
+PACK = 4
+GROUP = P * PACK
+HALF = 512
+LIST_COLS = HALF // 16
+WIDE = 1024
+N_TILES = N // P
+
+
+def tile_list_mask_titration_log_kernel(
+    tc, tab_words, tab_scales, offs, offs2, offs3, w1, depth, gain, wgs, page0, sc,
+    w4_words, w4_scales, w5, out_0, out_1, out_2, out_3,
+):
+    nc = tc.nc
+    with ExitStack() as ctx:
+        held = ctx.enter_context(tc.tile_pool(name="held", bufs=1))
+        ring = ctx.enter_context(tc.tile_pool(name="ring", bufs=2))
+        psum = ctx.enter_context(tc.psum_pool(name="psum", bufs=8))
+
+        def keep(name, shape, dtype):
+            return held.tile(shape, dtype, name=name, align_bytes=64)
+
+        def rotate(tag, bufs, shape, dtype):
+            return ring.tile(shape, dtype, name=tag, tag=tag, bufs=bufs, align_bytes=64)
+
+        page_rows = page0.rearrange("(b p t) c -> b t p c", p=P, t=PACK)
+        out_rows = out_1.rearrange("(b p t) c -> b t p c", p=P, t=PACK)
+
+        tab_s = keep("tab_s", [P, T], U8)
+        nc.gpsimd.memset(tab_s[:].bitcast(I32), 0)
+        w4_s = keep("w4_s", [P, 2, N], U8)
+        nc.vector.memset(w4_s[:].rearrange("p a n -> p (a n)").bitcast(I32), 0)
+        zero_in = keep("zero_in", [P, 1], F32)
+        nc.vector.memset(zero_in[:], 0.0)
+        zero = keep("zero", [P, 1], F32)
+        nc.scalar.activation(out=zero[:], in_=zero_in[:], func=ACT.Silu)
+
+        for q in range(4):
+            nc.gpsimd.dma_start(
+                out=tab_s[32 * q : 32 * q + 8, :].bitcast(I32),
+                in_=tab_scales[:, 4 * q : 4 * q + 4, :].bitcast(I32),
+            )
+        vec = {}
+        for name, src in (("depth", depth), ("gain", gain), ("sc", sc)):
+            vec[name] = keep(name, [P, 2, PACK], F32)
+            nc.scalar.dma_start(out=vec[name][:], in_=src.rearrange("(b p t) -> p b t", p=P, t=PACK))
+        half_depth = keep("half_depth", [P, 2, PACK], F32)
+        nc.gpsimd.tensor_scalar(half_depth[:], vec["depth"][:], 0.5, 0.0, ALU.mult, ALU.add)
+        neg2_gain = keep("neg2_gain", [P, 2, PACK], F32)
+        nc.gpsimd.tensor_scalar(neg2_gain[:], vec["gain"][:], -2.0, 0.0, ALU.mult, ALU.add)
+
+        w1_raw = {}
+
+        def load_w1(a, b):
+            w1_raw[a, b] = rotate("raw", 3, [P, PACK, GROUP], F32)
+            rows = w1[GROUP * a : GROUP * (a + 1), GROUP * b : GROUP * (b + 1)]
+            nc.sync.dma_start(out=w1_raw[a, b][:], in_=rows.rearrange("(p j) c -> p j c", j=PACK))
+
+        tab_w = {}
+
+        def load_tab(a):
+            tab_w[a] = rotate("wide", 2, [P, T], U32)
+            words = tab_words[a].rearrange("p t i -> p (t i)")
+            nc.sync.dma_start(out=tab_w[a][:].bitcast(I32), in_=words.bitcast(I32))
+
+        def load_list(name, src):
+            tile = held.tile([P, S // 16], U16, name=name)
+            nc.sync.dma_start(out=tile[:], in_=src)
+            return tile
+
+        pages = {}
+
+        def load_page(i):
+            pages[i] = rotate("page", 4, [P, T2], F32)
+            nc.sync.dma_start(out=pages[i][:], in_=page_rows[i // PACK, i % PACK])
+
+        wgs_rows = wgs.rearrange("(p t) s -> p t s", t=PACK)
+        wgs_first = keep("wgs_first", [P, S], F32)
+        wgs_rest = keep("wgs_rest", [P, PACK - 1, S], F32)
+
+        load_w1(0, 0)
+        list1 = load_list("list1", offs)
+        load_tab(0)
+        load_w1(1, 0)
+        for q in range(4):
+            nc.sync.dma_start(out=wgs_first[32 * q : 32 * q + 32, :], in_=wgs_rows[:, 0, :])
+        load_tab(1)
+        list2 = load_list("list2", offs2)
+        load_page(0)
+        list3 = load_list("list3", offs3)
+        for q in range(4):
+            nc.sync.dma_start(out=wgs_rest[32 * q : 32 * q + 32, :, :], in_=wgs_rows[:, 1:PACK, :])
+        load_page(1)
+        load_w1(0, 1)
+        load_w1(1, 1)
+        load_page(2)
+        load_page(3)
+        w5_raw = {}
+        for b in range(2):
+            w5_raw[b] = rotate("raw", 3, [P, PACK, N], F32) if b == 0 else rotate("xs", 2, [P, PACK, N], F32)
+            rows = w5[GROUP * b : GROUP * (b + 1), :]
+            nc.sync.dma_start(out=w5_raw[b][:], in_=rows.rearrange("(p j) c -> p j c", j=PACK))
+        w4_w = keep("w4_w", [P, 2, 2 * N], U8)
+        nc.sync.dma_start(out=w4_w[:].bitcast(I32), in_=w4_words.rearrange("a p c -> p a c").bitcast(I32))
+        for q in range(4):
+            nc.sync.dma_start(
+                out=w4_s[32 * q : 32 * q + 4, :, :].bitcast(I32),
+                in_=w4_scales[:, 4 * q : 4 * q + 4, :].rearrange("a r n -> r a n").bitcast(I32),
+            )
+
+        def copy_on(engine, out, in_):
+            if engine == "vector":
+                nc.vector.tensor_copy(out=out, in_=in_)
+            else:
+                nc.scalar.copy(out=out, in_=in_)
+
+        def interleave(planes, width, engine="scalar"):
+            grouped = rotate("bf", 4, [P, PACK * width], BF16)
+            copy_on(
+                engine,
+                grouped[:].rearrange("p (c i t) -> p c t i", i=4, t=PACK),
+                planes.rearrange("p t (c i) -> p c t i", i=4),
+            )
+            return grouped
+
+        def quantize(grouped, codes, scales):
+            nc.vector.quantize_mx(out=codes.bitcast(FP8X4), scales=scales, in_=grouped[:])
+
+        w1_c, w1_s = {}, {}
+
+        def prepare_w1(a, b):
+            grouped = rotate("bf", 4, [P, PACK * GROUP], BF16)
+            nc.scalar.copy(
+                out=grouped[:].rearrange("p (t m j) -> p m j t", t=PACK, j=PACK),
+                in_=w1_raw[a, b][:].rearrange("p j (m t) -> p m j t", t=PACK),
+            )
+            w1_c[a, b] = keep(f"w1_c{a}{b}", [P, GROUP], U32)
+            w1_s[a, b] = keep(f"w1_s{a}{b}", [P, GROUP], U8)
+            quantize(grouped, w1_c[a, b][:], w1_s[a, b][:])
+
+        w5_c = keep("w5_c", [P, 2, N], U32)
+        w5_s = keep("w5_s", [P, 2, N], U8)
+
+        def prepare_w5(b):
+            quantize(interleave(w5_raw[b][:], N), w5_c[:, b, :], w5_s[:, b, :])
+
+        v_w = [keep(f"v_w{a}", [P, S], U32) for a in range(2)]
+        v_s = keep("v_s", [P, S], U8)
+
+        def cols(jh):
+            return slice(HALF * jh, HALF * (jh + 1))
+
+        def entries(offsets, jh):
+            return offsets[:, LIST_COLS * jh : LIST_COLS * (jh + 1)]
+
+        h4, xs, picked, wide = {}, {}, {}, {}
+        h_c, h_s, x_c, x_s = {}, {}, {}, {}
+
+        def make_h(i):
+            b, t = divmod(i, PACK)
+            work = []
+            for jh in range(2):
+                acc = psum.tile([P, HALF], F32, name="bank", tag="bank")
+                for a in range(2):
+                    nc.tensor.matmul_mx(
+                        out=acc[:],
+                        lhsT=w1_c[a, b][:, P * t : P * (t + 1)].bitcast(FP8X4),
+                        lhsT_scale=w1_s[a, b][:, P * t : P * (t + 1)],
+                        rhs=v_w[a][:, cols(jh)].bitcast(FP8X4),
+                        rhs_scale=v_s[4 * a : P, cols(jh)],
+                        start=(a == 0),
+                        stop=(a == 1),
+                    )
+                tmp = rotate("tmp", 3, [P, HALF], F32)
+                nc.scalar.activation(out=tmp[:], in_=acc[:], func=ACT.Tanh, bias=zero[:])
+                work.append(tmp)
+            for tmp in work:
+                nc.scalar.activation(out=tmp[:], in_=tmp[:], func=ACT.Sin, scale=half_depth[:, b, t : t + 1])
+            for tmp in work:
+                nc.scalar.activation(out=tmp[:], in_=tmp[:], func=ACT.Square)
+            for jh, tmp in enumerate(work):
+                if t == 0:
+                    h4[b, jh] = rotate("h4", 3, [P, PACK, HALF], F32)
+                nc.scalar.activation(
+                    out=h4[b, jh][:, t, :], in_=tmp[:], func=ACT.Identity,
+                    scale=neg2_gain[:, b, t : t + 1], bias=vec["gain"][:, b, t : t + 1],
+                )
+
+        def change_page(i):
+            b, t = divmod(i, PACK)
+            weights = wgs_first[:] if t == 0 else wgs_rest[:, t - 1, :]
+            for jh in range(2):
+                nc.vector.tensor_tensor(
+                    pages[i][:].indirect(entries(list2, jh)), h4[b, jh][:, t, :], weights[:, cols(jh)], ALU.mult
+                )
+            for ch in range(2):
+                if t == 0:
+                    wide[b, ch] = rotate("wide", 2, [P, PACK, WIDE], F32)
+                nc.sync.dma_start(out=wide[b, ch][:, t, :], in_=pages[i][:, WIDE * ch : WIDE * (ch + 1)])
+            nc.sync.dma_start(out=out_rows[b, t], in_=pages[i][:])
+            picked[i] = rotate("picked", 2, [P, NP], F32)
+            nc.vector.tensor_copy(out=picked[i][:], in_=pages[i][:].indirect(list3[:]))
+            if i + 4 < 2 * PACK:
+                load_page(i + 4)
+
+        def scale_x(i):
+            b, t = divmod(i, PACK)
+            if t == 0:
+                xs[b] = rotate("xs", 2, [P, PACK, NP], BF16)
+            nc.scalar.activation(out=xs[b][:, t, :], in_=picked[i][:], func=ACT.Copy, scale=vec["sc"][:, b, t : t + 1])
+
+        def quantize_h(b):
+            for jh in range(2):
+                h_c[b, jh] = keep(f"h_c{b}{jh}", [P, HALF], U32)
+                h_s[b, jh] = keep(f"h_s{b}{jh}", [P, HALF], U8)
+                quantize(interleave(h4[b, jh][:], HALF), h_c[b, jh][:], h_s[b, jh][:])
+
+        def quantize_x(b, jh):
+            x_c[b, jh] = keep(f"x_c{b}{jh}", [P, HALF], U32)
+            x_s[b, jh] = keep(f"x_s{b}{jh}", [P, HALF], U8)
+            quantize(interleave(xs[b][:, :, cols(jh)], HALF), x_c[b, jh][:], x_s[b, jh][:])
+
+        plane_s = [keep(f"plane_s{b}", [P, T2], U8) for b in range(2)]
+
+        def quantize_page(b, ch, engines):
+            codes = rotate("plane_c", 2, [P, WIDE], U32)
+            for u in range(2):
+                grouped = interleave(wide[b, ch][:, :, cols(u)], HALF, engines[u])
+                c0 = WIDE * ch + HALF * u
+                quantize(grouped, codes[:, cols(u)], plane_s[b][:, c0 : c0 + HALF])
+            words = out_2[b].rearrange("p m t -> p (m t)").bitcast(I32)
+            nc.sync.dma_start(out=words[:, WIDE * ch : WIDE * (ch + 1)], in_=codes[:].bitcast(I32))
+            if ch == 1:
+                for q in range(4):
+                    nc.sync.dma_start(
+                        out=out_3[b, 4 * q : 4 * q + 4, :].bitcast(I32),
+                        in_=plane_s[b][32 * q : 32 * q + 4, :].bitcast(I32),
+                    )
+
+        sums = {}
+
+        def second_pass(kind, b, jh):
+            for n in range(N_TILES):
+                first = kind == "h" and b == 0
+                last = kind == "x" and b == 1
+                if first:
+                    sums[n, jh] = psum.tile([P, HALF], F32, name="bank", tag="bank")
+                if kind == "h":
+                    lhs = w5_c[:, b, P * n : P * (n + 1)].bitcast(FP8X4)
+                    lhs_s = w5_s[:, b, P * n : P * (n + 1)]
+                    rhs, rhs_s = h_c[b, jh], h_s[b, jh]
+                else:
+                    lhs = w4_w[:, b, 2 * P * n : 2 * P * (n + 1)].bitcast(FP4X4)
+                    lhs_s = w4_s[:, b, P * n : P * (n + 1)]
+                    rhs, rhs_s = x_c[b, jh], x_s[b, jh]
+                nc.tensor.matmul_mx(
+                    out=sums[n, jh][:], lhsT=lhs, lhsT_scale=lhs_s,
+                    rhs=rhs[:].bitcast(FP8X4), rhs_scale=rhs_s[:], start=first, stop=last,
+                )
+
+        def store_y(jh):
+            for n in range(N_TILES):
+                result = rotate("raw", 3, [P, HALF], F32)
+                nc.scalar.copy(out=result[:], in_=sums[n, jh][:])
+                nc.sync.dma_start(out=out_0[P * n : P * (n + 1), cols(jh)], in_=result[:])
+
+        prepare_w1(0, 0)
+        nc.vector.tensor_copy(out=v_w[0][:], in_=tab_w[0][:].indirect(list1[:]))
+        nc.vector.tensor_copy(out=v_s[:], in_=tab_s[:].indirect(list1[:]))
+        prepare_w1(1, 0)
+        for jh in range(2):
+            nc.vector.tensor_copy(out=v_w[1][:, cols(jh)], in_=tab_w[1][:].indirect(entries(list1, jh)))
+
+        make_h(0)
+        change_page(0)
+        make_h(1)
+        change_page(1)
+        prepare_w1(0, 1)
+        prepare_w1(1, 1)
+        make_h(2)
+        change_page(2)
+        scale_x(0)
+        prepare_w5(0)
+        prepare_w5(1)
+        make_h(3)
+        change_page(3)
+        scale_x(1)
+        quantize_h(0)
+        make_h(4)
+        change_page(4)
+        scale_x(2)
+        make_h(5)
+        change_page(5)
+        scale_x(3)
+        quantize_x(0, 0)
+        quantize_x(0, 1)
+        make_h(6)
+        change_page(6)
+        scale_x(4)
+        quantize_page(0, 0, ("scalar", "scalar"))
+        make_h(7)
+        change_page(7)
+        scale_x(5)
+        quantize_page(0, 1, ("scalar", "scalar"))
+        quantize_h(1)
+        scale_x(6)
+        scale_x(7)
+        for kind, b in (("h", 0), ("x", 0), ("h", 1)):
+            for jh in range(2):
+                second_pass(kind, b, jh)
+        quantize_page(1, 0, ("vector", "vector"))
+        for jh in range(2):
+            quantize_x(1, jh)
+            second_pass("x", 1, jh)
+        store_y(0)
+        quantize_page(1, 1, ("vector", "scalar"))
+        store_y(1)

@@ -22,6 +22,7 @@ GROUP = P * PACK
 HALF = 512
 LIST_COLS = HALF // 16
 WIDE = 1024
+PAGES = 5
 N_TILES = N // P
 
 
@@ -70,7 +71,7 @@ def tile_list_mask_titration_log_kernel(
         w1_raw = {}
 
         def load_w1(a, b):
-            w1_raw[a, b] = rotate("raw", 3, [P, PACK, GROUP], F32)
+            w1_raw[a, b] = rotate("raw", 2, [P, PACK, GROUP], F32)
             rows = w1[GROUP * a : GROUP * (a + 1), GROUP * b : GROUP * (b + 1)]
             nc.sync.dma_start(out=w1_raw[a, b][:], in_=rows.rearrange("(p j) c -> p j c", j=PACK))
 
@@ -89,7 +90,7 @@ def tile_list_mask_titration_log_kernel(
         pages = {}
 
         def load_page(i):
-            pages[i] = rotate("page", 4, [P, T2], F32)
+            pages[i] = rotate("page", PAGES, [P, T2], F32)
             nc.sync.dma_start(out=pages[i][:], in_=page_rows[i // PACK, i % PACK])
 
         wgs_rows = wgs.rearrange("(p t) s -> p t s", t=PACK)
@@ -100,22 +101,23 @@ def tile_list_mask_titration_log_kernel(
         list1 = load_list("list1", offs)
         load_tab(0)
         load_w1(1, 0)
-        for q in range(4):
+        for q in (0, 2, 1, 3):
             nc.sync.dma_start(out=wgs_first[32 * q : 32 * q + 32, :], in_=wgs_rows[:, 0, :])
         load_tab(1)
         list2 = load_list("list2", offs2)
         load_page(0)
         list3 = load_list("list3", offs3)
-        for q in range(4):
+        for q in (0, 2, 1, 3):
             nc.sync.dma_start(out=wgs_rest[32 * q : 32 * q + 32, :, :], in_=wgs_rows[:, 1:PACK, :])
         load_page(1)
         load_w1(0, 1)
         load_w1(1, 1)
         load_page(2)
         load_page(3)
+        load_page(4)
         w5_raw = {}
         for b in range(2):
-            w5_raw[b] = rotate("raw", 3, [P, PACK, N], F32) if b == 0 else rotate("xs", 2, [P, PACK, N], F32)
+            w5_raw[b] = rotate(f"xs{b}", 1, [P, PACK, N], F32)
             rows = w5[GROUP * b : GROUP * (b + 1), :]
             nc.sync.dma_start(out=w5_raw[b][:], in_=rows.rearrange("(p j) c -> p j c", j=PACK))
         w4_w = keep("w4_w", [P, 2, 2 * N], U8)
@@ -132,12 +134,13 @@ def tile_list_mask_titration_log_kernel(
             else:
                 nc.scalar.copy(out=out, in_=in_)
 
-        def interleave(planes, width, engine="scalar"):
-            grouped = rotate("bf", 4, [P, PACK * width], BF16)
+        def interleave(planes, width, engine="scalar", grouped=None):
+            if grouped is None:
+                grouped = rotate("bf", 4, [P, PACK * width], BF16)
             copy_on(
                 engine,
-                grouped[:].rearrange("p (c i t) -> p c t i", i=4, t=PACK),
-                planes.rearrange("p t (c i) -> p c t i", i=4),
+                grouped[:].rearrange("p (c i t) -> p c t i", i=2, t=PACK),
+                planes.rearrange("p t (c i) -> p c t i", i=2),
             )
             return grouped
 
@@ -149,8 +152,8 @@ def tile_list_mask_titration_log_kernel(
         def prepare_w1(a, b):
             grouped = rotate("bf", 4, [P, PACK * GROUP], BF16)
             nc.scalar.copy(
-                out=grouped[:].rearrange("p (t m j) -> p m j t", t=PACK, j=PACK),
-                in_=w1_raw[a, b][:].rearrange("p j (m t) -> p m j t", t=PACK),
+                out=grouped[:].rearrange("p (t m j) -> p m t j", t=PACK, j=PACK),
+                in_=w1_raw[a, b][:].rearrange("p j (m t) -> p m t j", t=PACK),
             )
             w1_c[a, b] = keep(f"w1_c{a}{b}", [P, GROUP], U32)
             w1_s[a, b] = keep(f"w1_s{a}{b}", [P, GROUP], U8)
@@ -174,10 +177,10 @@ def tile_list_mask_titration_log_kernel(
         h4, xs, picked, wide = {}, {}, {}, {}
         h_c, h_s, x_c, x_s = {}, {}, {}, {}
 
-        def make_h(i):
+        def make_h(i, halves=(0, 1), pieces=1, between=None):
             b, t = divmod(i, PACK)
             work = []
-            for jh in range(2):
+            for jh in halves:
                 acc = psum.tile([P, HALF], F32, name="bank", tag="bank")
                 for a in range(2):
                     nc.tensor.matmul_mx(
@@ -190,42 +193,60 @@ def tile_list_mask_titration_log_kernel(
                         stop=(a == 1),
                     )
                 tmp = rotate("tmp", 3, [P, HALF], F32)
-                nc.scalar.activation(out=tmp[:], in_=acc[:], func=ACT.Tanh, bias=zero[:])
-                work.append(tmp)
-            for tmp in work:
-                nc.scalar.activation(out=tmp[:], in_=tmp[:], func=ACT.Sin, scale=half_depth[:, b, t : t + 1])
-            for tmp in work:
-                nc.scalar.activation(out=tmp[:], in_=tmp[:], func=ACT.Square)
-            for jh, tmp in enumerate(work):
                 if t == 0:
                     h4[b, jh] = rotate("h4", 3, [P, PACK, HALF], F32)
+                for c0 in range(0, HALF, HALF // pieces):
+                    part = slice(c0, c0 + HALF // pieces)
+                    nc.scalar.activation(out=tmp[:, part], in_=acc[:, part], func=ACT.Tanh, bias=zero[:])
+                    work.append((tmp[:, part], h4[b, jh][:, t, part]))
+            for tmp, dest in work:
+                nc.scalar.activation(out=tmp, in_=tmp, func=ACT.Sin, scale=half_depth[:, b, t : t + 1])
+            for tmp, dest in work:
+                nc.scalar.activation(out=tmp, in_=tmp, func=ACT.Square)
+            for k, (tmp, dest) in enumerate(work):
                 nc.scalar.activation(
-                    out=h4[b, jh][:, t, :], in_=tmp[:], func=ACT.Identity,
+                    out=dest, in_=tmp, func=ACT.Identity,
                     scale=neg2_gain[:, b, t : t + 1], bias=vec["gain"][:, b, t : t + 1],
                 )
+                if k == 0 and between is not None:
+                    scale_x(between)
+
+        def put(i, jh):
+            b, t = divmod(i, PACK)
+            weights = wgs_first[:] if t == 0 else wgs_rest[:, t - 1, :]
+            nc.vector.tensor_tensor(
+                pages[i][:].indirect(entries(list2, jh)), h4[b, jh][:, t, :], weights[:, cols(jh)], ALU.mult
+            )
+
+        def pick(i, halves=False):
+            picked[i] = rotate("picked", 2, [P, NP], F32)
+            if halves:
+                for jh in range(2):
+                    nc.vector.tensor_copy(out=picked[i][:, cols(jh)], in_=pages[i][:].indirect(entries(list3, jh)))
+            else:
+                nc.vector.tensor_copy(out=picked[i][:], in_=pages[i][:].indirect(list3[:]))
+            if i + PAGES < 2 * PACK:
+                load_page(i + PAGES)
 
         def change_page(i):
             b, t = divmod(i, PACK)
-            weights = wgs_first[:] if t == 0 else wgs_rest[:, t - 1, :]
-            for jh in range(2):
-                nc.vector.tensor_tensor(
-                    pages[i][:].indirect(entries(list2, jh)), h4[b, jh][:, t, :], weights[:, cols(jh)], ALU.mult
-                )
+            put(i, 0)
+            if i > 0:
+                pick(i - 1)
+            put(i, 1)
             for ch in range(2):
                 if t == 0:
                     wide[b, ch] = rotate("wide", 2, [P, PACK, WIDE], F32)
                 nc.sync.dma_start(out=wide[b, ch][:, t, :], in_=pages[i][:, WIDE * ch : WIDE * (ch + 1)])
             nc.sync.dma_start(out=out_rows[b, t], in_=pages[i][:])
-            picked[i] = rotate("picked", 2, [P, NP], F32)
-            nc.vector.tensor_copy(out=picked[i][:], in_=pages[i][:].indirect(list3[:]))
-            if i + 4 < 2 * PACK:
-                load_page(i + 4)
 
-        def scale_x(i):
+        def scale_x(i, part=slice(0, NP)):
             b, t = divmod(i, PACK)
             if t == 0:
-                xs[b] = rotate("xs", 2, [P, PACK, NP], BF16)
-            nc.scalar.activation(out=xs[b][:, t, :], in_=picked[i][:], func=ACT.Copy, scale=vec["sc"][:, b, t : t + 1])
+                xs[b] = rotate(f"xs{b}", 1, [P, PACK, NP], BF16)
+            nc.scalar.activation(
+                out=xs[b][:, t, part], in_=picked[i][:, part], func=ACT.Copy, scale=vec["sc"][:, b, t : t + 1]
+            )
 
         def quantize_h(b):
             for jh in range(2):
@@ -233,21 +254,26 @@ def tile_list_mask_titration_log_kernel(
                 h_s[b, jh] = keep(f"h_s{b}{jh}", [P, HALF], U8)
                 quantize(interleave(h4[b, jh][:], HALF), h_c[b, jh][:], h_s[b, jh][:])
 
-        def quantize_x(b, jh):
+        def quantize_x(b, jh, engine="scalar"):
             x_c[b, jh] = keep(f"x_c{b}{jh}", [P, HALF], U32)
             x_s[b, jh] = keep(f"x_s{b}{jh}", [P, HALF], U8)
-            quantize(interleave(xs[b][:, :, cols(jh)], HALF), x_c[b, jh][:], x_s[b, jh][:])
+            quantize(interleave(xs[b][:, :, cols(jh)], HALF, engine), x_c[b, jh][:], x_s[b, jh][:])
 
         plane_s = [keep(f"plane_s{b}", [P, T2], U8) for b in range(2)]
 
         def quantize_page(b, ch, engines):
             codes = rotate("plane_c", 2, [P, WIDE], U32)
+            words = out_2[b].rearrange("p m t -> p (m t)").bitcast(I32)
+            if (b, ch) == (1, 1):
+                both = rotate("xs1", 1, [P, PACK * WIDE], BF16)
+            else:
+                both = rotate("raw", 2, [P, PACK * WIDE], BF16)
             for u in range(2):
-                grouped = interleave(wide[b, ch][:, :, cols(u)], HALF, engines[u])
+                part = both[:, PACK * HALF * u : PACK * HALF * (u + 1)]
+                grouped = interleave(wide[b, ch][:, :, cols(u)], HALF, engines[u], part)
                 c0 = WIDE * ch + HALF * u
                 quantize(grouped, codes[:, cols(u)], plane_s[b][:, c0 : c0 + HALF])
-            words = out_2[b].rearrange("p m t -> p (m t)").bitcast(I32)
-            nc.sync.dma_start(out=words[:, WIDE * ch : WIDE * (ch + 1)], in_=codes[:].bitcast(I32))
+                nc.sync.dma_start(out=words[:, c0 : c0 + HALF], in_=codes[:, cols(u)].bitcast(I32))
             if ch == 1:
                 for q in range(4):
                     nc.sync.dma_start(
@@ -276,11 +302,13 @@ def tile_list_mask_titration_log_kernel(
                     rhs=rhs[:].bitcast(FP8X4), rhs_scale=rhs_s[:], start=first, stop=last,
                 )
 
-        def store_y(jh):
-            for n in range(N_TILES):
-                result = rotate("raw", 3, [P, HALF], F32)
-                nc.scalar.copy(out=result[:], in_=sums[n, jh][:])
-                nc.sync.dma_start(out=out_0[P * n : P * (n + 1), cols(jh)], in_=result[:])
+        def store_y():
+            result = rotate("wide", 2, [P, 2 * N_TILES * HALF], F32)
+            for jh in range(2):
+                for n in range(N_TILES):
+                    part = result[:, cols(N_TILES * jh + n)]
+                    nc.scalar.copy(out=part, in_=sums[n, jh][:])
+                    nc.scalar.dma_start(out=out_0[P * n : P * (n + 1), cols(jh)], in_=part)
 
         prepare_w1(0, 0)
         nc.vector.tensor_copy(out=v_w[0][:], in_=tab_w[0][:].indirect(list1[:]))
@@ -289,7 +317,8 @@ def tile_list_mask_titration_log_kernel(
         for jh in range(2):
             nc.vector.tensor_copy(out=v_w[1][:, cols(jh)], in_=tab_w[1][:].indirect(entries(list1, jh)))
 
-        make_h(0)
+        make_h(0, (0,), 2)
+        make_h(0, (1,), 2)
         change_page(0)
         make_h(1)
         change_page(1)
@@ -297,39 +326,34 @@ def tile_list_mask_titration_log_kernel(
         prepare_w1(1, 1)
         make_h(2)
         change_page(2)
-        scale_x(0)
         prepare_w5(0)
         prepare_w5(1)
-        make_h(3)
+        make_h(3, between=0)
         change_page(3)
-        scale_x(1)
         quantize_h(0)
-        make_h(4)
+        make_h(4, between=1)
         change_page(4)
-        scale_x(2)
-        make_h(5)
+        make_h(5, between=2)
         change_page(5)
-        scale_x(3)
+        quantize_page(0, 0, ("scalar", "scalar"))
+        make_h(6, between=3)
+        change_page(6)
+        quantize_page(0, 1, ("scalar", "scalar"))
+        make_h(7, between=4)
+        change_page(7)
         quantize_x(0, 0)
         quantize_x(0, 1)
-        make_h(6)
-        change_page(6)
-        scale_x(4)
-        quantize_page(0, 0, ("scalar", "scalar"))
-        make_h(7)
-        change_page(7)
         scale_x(5)
-        quantize_page(0, 1, ("scalar", "scalar"))
         quantize_h(1)
+        pick(7, halves=True)
         scale_x(6)
-        scale_x(7)
         for kind, b in (("h", 0), ("x", 0), ("h", 1)):
             for jh in range(2):
                 second_pass(kind, b, jh)
-        quantize_page(1, 0, ("vector", "vector"))
         for jh in range(2):
-            quantize_x(1, jh)
+            scale_x(7, cols(jh))
+            quantize_x(1, jh, "vector")
             second_pass("x", 1, jh)
-        store_y(0)
-        quantize_page(1, 1, ("vector", "scalar"))
-        store_y(1)
+        quantize_page(1, 0, ("scalar", "scalar"))
+        quantize_page(1, 1, ("vector", "vector"))
+        store_y()

@@ -23,6 +23,7 @@ HALF = 512
 LIST_COLS = HALF // 16
 WIDE = 1024
 PAGES = 5
+LATE_PAGE_TAGS = {5: "tab_s", 6: "v_w", 7: "w1_c"}
 N_TILES = N // P
 
 
@@ -45,7 +46,7 @@ def tile_list_mask_titration_log_kernel(
         page_rows = page0.rearrange("(b p t) c -> b t p c", p=P, t=PACK)
         out_rows = out_1.rearrange("(b p t) c -> b t p c", p=P, t=PACK)
 
-        tab_s = keep("tab_s", [P, T], U8)
+        tab_s = rotate("tab_s", 1, [P, T], U8)
         nc.gpsimd.memset(tab_s[:].bitcast(I32), 0)
         w4_s = keep("w4_s", [P, 2, N], U8)
         nc.vector.memset(w4_s[:].rearrange("p a n -> p (a n)").bitcast(I32), 0)
@@ -78,7 +79,7 @@ def tile_list_mask_titration_log_kernel(
         tab_w = {}
 
         def load_tab(a):
-            tab_w[a] = rotate("wide", 2, [P, T], U32)
+            tab_w[a] = rotate(f"wide{a}", 1, [P, T], U32)
             words = tab_words[a].rearrange("p t i -> p (t i)")
             nc.sync.dma_start(out=tab_w[a][:].bitcast(I32), in_=words.bitcast(I32))
 
@@ -90,7 +91,10 @@ def tile_list_mask_titration_log_kernel(
         pages = {}
 
         def load_page(i):
-            pages[i] = rotate("page", PAGES, [P, T2], F32)
+            if i in LATE_PAGE_TAGS:
+                pages[i] = rotate(LATE_PAGE_TAGS[i], 1, [P, T2], F32)
+            else:
+                pages[i] = rotate("page", PAGES, [P, T2], F32)
             nc.sync.dma_start(out=pages[i][:], in_=page_rows[i // PACK, i % PACK])
 
         wgs_rows = wgs.rearrange("(p t) s -> p t s", t=PACK)
@@ -107,26 +111,27 @@ def tile_list_mask_titration_log_kernel(
         list2 = load_list("list2", offs2)
         load_page(0)
         list3 = load_list("list3", offs3)
+        load_w1(0, 1)
+        load_w1(1, 1)
         for q in (0, 2, 1, 3):
             nc.sync.dma_start(out=wgs_rest[32 * q : 32 * q + 32, :, :], in_=wgs_rows[:, 1:PACK, :])
         load_page(1)
-        load_w1(0, 1)
-        load_w1(1, 1)
-        load_page(2)
-        load_page(3)
-        load_page(4)
         w5_raw = {}
-        for b in range(2):
-            w5_raw[b] = rotate(f"xs{b}", 1, [P, PACK, N], F32)
-            rows = w5[GROUP * b : GROUP * (b + 1), :]
-            nc.sync.dma_start(out=w5_raw[b][:], in_=rows.rearrange("(p j) c -> p j c", j=PACK))
         w4_w = keep("w4_w", [P, 2, 2 * N], U8)
-        nc.sync.dma_start(out=w4_w[:].bitcast(I32), in_=w4_words.rearrange("a p c -> p a c").bitcast(I32))
-        for q in range(4):
-            nc.sync.dma_start(
-                out=w4_s[32 * q : 32 * q + 4, :, :].bitcast(I32),
-                in_=w4_scales[:, 4 * q : 4 * q + 4, :].rearrange("a r n -> r a n").bitcast(I32),
-            )
+
+        def load_w5():
+            for b in range(2):
+                w5_raw[b] = rotate(("tab_s", "xs1")[b], 1, [P, PACK, N], F32)
+                rows = w5[GROUP * b : GROUP * (b + 1), :]
+                nc.sync.dma_start(out=w5_raw[b][:], in_=rows.rearrange("(p j) c -> p j c", j=PACK))
+
+        def load_w4():
+            nc.sync.dma_start(out=w4_w[:].bitcast(I32), in_=w4_words.rearrange("a p c -> p a c").bitcast(I32))
+            for q in range(4):
+                nc.sync.dma_start(
+                    out=w4_s[32 * q : 32 * q + 4, :, :].bitcast(I32),
+                    in_=w4_scales[:, 4 * q : 4 * q + 4, :].rearrange("a r n -> r a n").bitcast(I32),
+                )
 
         def copy_on(engine, out, in_):
             if engine == "vector":
@@ -148,14 +153,16 @@ def tile_list_mask_titration_log_kernel(
             nc.vector.quantize_mx(out=codes.bitcast(FP8X4), scales=scales, in_=grouped[:])
 
         w1_c, w1_s = {}, {}
+        w1_all = rotate("w1_c", 1, [P, 4 * GROUP], U32)
 
-        def prepare_w1(a, b):
+        def prepare_w1(a, b, engine="scalar"):
             grouped = rotate("bf", 4, [P, PACK * GROUP], BF16)
-            nc.scalar.copy(
-                out=grouped[:].rearrange("p (t m j) -> p m t j", t=PACK, j=PACK),
-                in_=w1_raw[a, b][:].rearrange("p j (m t) -> p m t j", t=PACK),
+            copy_on(
+                engine,
+                grouped[:].rearrange("p (t m j) -> p m t j", t=PACK, j=PACK),
+                w1_raw[a, b][:].rearrange("p j (m t) -> p m t j", t=PACK),
             )
-            w1_c[a, b] = keep(f"w1_c{a}{b}", [P, GROUP], U32)
+            w1_c[a, b] = w1_all[:, GROUP * (2 * b + a) : GROUP * (2 * b + a + 1)]
             w1_s[a, b] = keep(f"w1_s{a}{b}", [P, GROUP], U8)
             quantize(grouped, w1_c[a, b][:], w1_s[a, b][:])
 
@@ -163,9 +170,10 @@ def tile_list_mask_titration_log_kernel(
         w5_s = keep("w5_s", [P, 2, N], U8)
 
         def prepare_w5(b):
-            quantize(interleave(w5_raw[b][:], N), w5_c[:, b, :], w5_s[:, b, :])
+            quantize(interleave(w5_raw[b][:], N, "vector"), w5_c[:, b, :], w5_s[:, b, :])
 
-        v_w = [keep(f"v_w{a}", [P, S], U32) for a in range(2)]
+        v_both = rotate("v_w", 1, [P, 2 * S], U32)
+        v_w = [v_both[:, S * a : S * (a + 1)] for a in range(2)]
         v_s = keep("v_s", [P, S], U8)
 
         def cols(jh):
@@ -225,20 +233,24 @@ def tile_list_mask_titration_log_kernel(
                     nc.vector.tensor_copy(out=picked[i][:, cols(jh)], in_=pages[i][:].indirect(entries(list3, jh)))
             else:
                 nc.vector.tensor_copy(out=picked[i][:], in_=pages[i][:].indirect(list3[:]))
-            if i + PAGES < 2 * PACK:
-                load_page(i + PAGES)
 
         def change_page(i):
-            b, t = divmod(i, PACK)
             put(i, 0)
             if i > 0:
                 pick(i - 1)
             put(i, 1)
-            for ch in range(2):
-                if t == 0:
-                    wide[b, ch] = rotate("wide", 2, [P, PACK, WIDE], F32)
-                nc.sync.dma_start(out=wide[b, ch][:, t, :], in_=pages[i][:, WIDE * ch : WIDE * (ch + 1)])
-            nc.sync.dma_start(out=out_rows[b, t], in_=pages[i][:])
+            spread(i, 0)
+            spread(i, 1)
+
+        def spread(i, ch):
+            b, t = divmod(i, PACK)
+            if t == 0:
+                wide[b, ch] = rotate(f"wide{ch}", 1, [P, PACK, WIDE], F32)
+            nc.sync.dma_start(out=wide[b, ch][:, t, :], in_=pages[i][:, WIDE * ch : WIDE * (ch + 1)])
+
+        def store_page(i):
+            queue = nc.gpsimd if PACK <= i < 2 * PACK - 1 else nc.sync
+            queue.dma_start(out=out_rows[i // PACK, i % PACK], in_=pages[i][:])
 
         def scale_x(i, part=slice(0, NP)):
             b, t = divmod(i, PACK)
@@ -259,9 +271,10 @@ def tile_list_mask_titration_log_kernel(
             x_s[b, jh] = keep(f"x_s{b}{jh}", [P, HALF], U8)
             quantize(interleave(xs[b][:, :, cols(jh)], HALF, engine), x_c[b, jh][:], x_s[b, jh][:])
 
-        plane_s = [keep(f"plane_s{b}", [P, T2], U8) for b in range(2)]
+        plane_s = keep("plane_s", [P, T2], U8)
 
         def quantize_page(b, ch, engines):
+            queue = nc.gpsimd if b == 0 else nc.sync
             codes = rotate("plane_c", 2, [P, WIDE], U32)
             words = out_2[b].rearrange("p m t -> p (m t)").bitcast(I32)
             if (b, ch) == (1, 1):
@@ -272,13 +285,13 @@ def tile_list_mask_titration_log_kernel(
                 part = both[:, PACK * HALF * u : PACK * HALF * (u + 1)]
                 grouped = interleave(wide[b, ch][:, :, cols(u)], HALF, engines[u], part)
                 c0 = WIDE * ch + HALF * u
-                quantize(grouped, codes[:, cols(u)], plane_s[b][:, c0 : c0 + HALF])
-                nc.sync.dma_start(out=words[:, c0 : c0 + HALF], in_=codes[:, cols(u)].bitcast(I32))
+                quantize(grouped, codes[:, cols(u)], plane_s[4 * b : P, c0 : c0 + HALF])
+            queue.dma_start(out=words[:, WIDE * ch : WIDE * (ch + 1)], in_=codes[:].bitcast(I32))
             if ch == 1:
                 for q in range(4):
-                    nc.sync.dma_start(
+                    queue.dma_start(
                         out=out_3[b, 4 * q : 4 * q + 4, :].bitcast(I32),
-                        in_=plane_s[b][32 * q : 32 * q + 4, :].bitcast(I32),
+                        in_=plane_s[32 * q + 4 * b : 32 * q + 4 * b + 4, :].bitcast(I32),
                     )
 
         sums = {}
@@ -303,12 +316,16 @@ def tile_list_mask_titration_log_kernel(
                 )
 
         def store_y():
-            result = rotate("wide", 2, [P, 2 * N_TILES * HALF], F32)
+            result = rotate("wide0", 1, [P, 2 * N_TILES * HALF], F32)
             for jh in range(2):
                 for n in range(N_TILES):
                     part = result[:, cols(N_TILES * jh + n)]
                     nc.scalar.copy(out=part, in_=sums[n, jh][:])
-                    nc.scalar.dma_start(out=out_0[P * n : P * (n + 1), cols(jh)], in_=part)
+                written = result[:, N_TILES * HALF * jh : N_TILES * HALF * (jh + 1)]
+                nc.scalar.dma_start(
+                    out=out_0[:, cols(jh)].rearrange("(n p) c -> p n c", p=P),
+                    in_=written.rearrange("p (n c) -> p n c", n=N_TILES),
+                )
 
         prepare_w1(0, 0)
         nc.vector.tensor_copy(out=v_w[0][:], in_=tab_w[0][:].indirect(list1[:]))
@@ -317,6 +334,10 @@ def tile_list_mask_titration_log_kernel(
         for jh in range(2):
             nc.vector.tensor_copy(out=v_w[1][:, cols(jh)], in_=tab_w[1][:].indirect(entries(list1, jh)))
 
+        load_page(2)
+        load_w5()
+        load_page(3)
+        load_page(4)
         make_h(0, (0,), 2)
         make_h(0, (1,), 2)
         change_page(0)
@@ -328,24 +349,36 @@ def tile_list_mask_titration_log_kernel(
         change_page(2)
         prepare_w5(0)
         prepare_w5(1)
+        load_page(5)
         make_h(3, between=0)
         change_page(3)
+        load_page(6)
+        load_page(7)
+        load_w4()
         quantize_h(0)
         make_h(4, between=1)
         change_page(4)
         make_h(5, between=2)
         change_page(5)
         quantize_page(0, 0, ("scalar", "scalar"))
+        store_page(0)
+        store_page(1)
+        store_page(2)
         make_h(6, between=3)
         change_page(6)
         quantize_page(0, 1, ("scalar", "scalar"))
+        store_page(3)
+        store_page(4)
+        store_page(5)
         make_h(7, between=4)
+        store_page(6)
         change_page(7)
         quantize_x(0, 0)
         quantize_x(0, 1)
         scale_x(5)
         quantize_h(1)
         pick(7, halves=True)
+        store_page(7)
         scale_x(6)
         for kind, b in (("h", 0), ("x", 0), ("h", 1)):
             for jh in range(2):

@@ -111,17 +111,17 @@ def tile_list_mask_titration_log_kernel(
         list2 = load_list("list2", offs2)
         load_page(0)
         list3 = load_list("list3", offs3)
-        load_w1(0, 1)
-        load_w1(1, 1)
         for q in (0, 2, 1, 3):
             nc.sync.dma_start(out=wgs_rest[32 * q : 32 * q + 32, :, :], in_=wgs_rows[:, 1:PACK, :])
         load_page(1)
+        load_w1(0, 1)
+        load_w1(1, 1)
         w5_raw = {}
         w4_w = keep("w4_w", [P, 2, 2 * N], U8)
 
         def load_w5():
             for b in range(2):
-                w5_raw[b] = rotate(("tab_s", "xs1")[b], 1, [P, PACK, N], F32)
+                w5_raw[b] = rotate(f"xs{b}", 1, [P, PACK, N], F32)
                 rows = w5[GROUP * b : GROUP * (b + 1), :]
                 nc.sync.dma_start(out=w5_raw[b][:], in_=rows.rearrange("(p j) c -> p j c", j=PACK))
 
@@ -142,11 +142,15 @@ def tile_list_mask_titration_log_kernel(
         def interleave(planes, width, engine="scalar", grouped=None):
             if grouped is None:
                 grouped = rotate("bf", 4, [P, PACK * width], BF16)
-            copy_on(
-                engine,
-                grouped[:].rearrange("p (c i t) -> p c t i", i=2, t=PACK),
-                planes.rearrange("p t (c i) -> p c t i", i=2),
-            )
+            if engine == "vector":
+                nc.vector.tensor_copy(
+                    out=grouped[:].rearrange("p (c t) -> p c t", t=PACK), in_=planes.rearrange("p t c -> p c t")
+                )
+            else:
+                nc.scalar.copy(
+                    out=grouped[:].rearrange("p (c i t) -> p c t i", i=4, t=PACK),
+                    in_=planes.rearrange("p t (c i) -> p c t i", i=4),
+                )
             return grouped
 
         def quantize(grouped, codes, scales):
@@ -159,8 +163,8 @@ def tile_list_mask_titration_log_kernel(
             grouped = rotate("bf", 4, [P, PACK * GROUP], BF16)
             copy_on(
                 engine,
-                grouped[:].rearrange("p (t m j) -> p m t j", t=PACK, j=PACK),
-                w1_raw[a, b][:].rearrange("p j (m t) -> p m t j", t=PACK),
+                grouped[:].rearrange("p (t m j) -> p m j t", t=PACK, j=PACK),
+                w1_raw[a, b][:].rearrange("p j (m t) -> p m j t", t=PACK),
             )
             w1_c[a, b] = w1_all[:, GROUP * (2 * b + a) : GROUP * (2 * b + a + 1)]
             w1_s[a, b] = keep(f"w1_s{a}{b}", [P, GROUP], U8)
@@ -170,7 +174,7 @@ def tile_list_mask_titration_log_kernel(
         w5_s = keep("w5_s", [P, 2, N], U8)
 
         def prepare_w5(b):
-            quantize(interleave(w5_raw[b][:], N, "vector"), w5_c[:, b, :], w5_s[:, b, :])
+            quantize(interleave(w5_raw[b][:], N), w5_c[:, b, :], w5_s[:, b, :])
 
         v_both = rotate("v_w", 1, [P, 2 * S], U32)
         v_w = [v_both[:, S * a : S * (a + 1)] for a in range(2)]
@@ -385,7 +389,7 @@ def tile_list_mask_titration_log_kernel(
                 second_pass(kind, b, jh)
         for jh in range(2):
             scale_x(7, cols(jh))
-            quantize_x(1, jh, "vector")
+            quantize_x(1, jh, ("scalar", "vector")[jh])
             second_pass("x", 1, jh)
         quantize_page(1, 0, ("scalar", "scalar"))
         quantize_page(1, 1, ("vector", "vector"))

from contextlib import ExitStack

import concourse.mybir as mybir

K, T, S, H, T2, NP, N = 1024, 4096, 1024, 1024, 2048, 1024, 384
FLOPS = 2 * K * H * S + 2 * 2 * H * N * NP

F32 = mybir.dt.float32
BF16 = mybir.dt.bfloat16
I32 = mybir.dt.int32
U32 = mybir.dt.uint32
U16 = mybir.dt.uint16
U8 = mybir.dt.uint8
FP8X4 = mybir.dt.float8_e4m3fn_x4
FP4X4 = mybir.dt.float4_e2m1fn_x4
ACT = mybir.ActivationFunctionType
ALU = mybir.AluOpType

P = 128
PACK = 4
GROUP = P * PACK
HALF = 512
LIST_COLS = HALF // 16
WIDE = 1024
PAGES = 5
LATE_PAGE_TAGS = {5: "tab_s", 6: "v_w", 7: "w1_c"}
N_TILES = N // P


def tile_list_mask_titration_log_kernel(
    tc, tab_words, tab_scales, offs, offs2, offs3, w1, depth, gain, wgs, page0, sc,
    w4_words, w4_scales, w5, out_0, out_1, out_2, out_3,
):
    nc = tc.nc
    with ExitStack() as ctx:
        held = ctx.enter_context(tc.tile_pool(name="held", bufs=1))
        ring = ctx.enter_context(tc.tile_pool(name="ring", bufs=2))
        psum = ctx.enter_context(tc.psum_pool(name="psum", bufs=8))

        def keep(name, shape, dtype):
            return held.tile(shape, dtype, name=name, align_bytes=64)

        def rotate(tag, bufs, shape, dtype):
            return ring.tile(shape, dtype, name=tag, tag=tag, bufs=bufs, align_bytes=64)

        page_rows = page0.rearrange("(b p t) c -> b t p c", p=P, t=PACK)
        out_rows = out_1.rearrange("(b p t) c -> b t p c", p=P, t=PACK)

        tab_s = rotate("tab_s", 1, [P, T], U8)
        nc.gpsimd.memset(tab_s[:].bitcast(I32), 0)
        w4_s = keep("w4_s", [P, 2, N], U8)
        nc.vector.memset(w4_s[:].rearrange("p a n -> p (a n)").bitcast(I32), 0)
        zero_in = keep("zero_in", [P, 1], F32)
        nc.vector.memset(zero_in[:], 0.0)
        zero = keep("zero", [P, 1], F32)
        nc.scalar.activation(out=zero[:], in_=zero_in[:], func=ACT.Silu)

        for q in range(4):
            nc.gpsimd.dma_start(
                out=tab_s[32 * q : 32 * q + 8, :].bitcast(I32),
                in_=tab_scales[:, 4 * q : 4 * q + 4, :].bitcast(I32),
            )
        vec = {}
        for name, src in (("depth", depth), ("gain", gain), ("sc", sc)):
            vec[name] = keep(name, [P, 2, PACK], F32)
            nc.scalar.dma_start(out=vec[name][:], in_=src.rearrange("(b p t) -> p b t", p=P, t=PACK))
        half_depth = keep("half_depth", [P, 2, PACK], F32)
        nc.gpsimd.tensor_scalar(half_depth[:], vec["depth"][:], 0.5, 0.0, ALU.mult, ALU.add)
        neg2_gain = keep("neg2_gain", [P, 2, PACK], F32)
        nc.gpsimd.tensor_scalar(neg2_gain[:], vec["gain"][:], -2.0, 0.0, ALU.mult, ALU.add)

        w1_raw = {}

        def load_w1(a, b):
            w1_raw[a, b] = rotate("raw", 2, [P, PACK, GROUP], F32)
            rows = w1[GROUP * a : GROUP * (a + 1), GROUP * b : GROUP * (b + 1)]
            nc.sync.dma_start(out=w1_raw[a, b][:], in_=rows.rearrange("(p j) c -> p j c", j=PACK))

        tab_w = {}

        def load_tab(a):
            tab_w[a] = rotate(f"wide{a}", 1, [P, T], U32)
            words = tab_words[a].rearrange("p t i -> p (t i)")
            nc.sync.dma_start(out=tab_w[a][:].bitcast(I32), in_=words.bitcast(I32))

        def load_list(name, src):
            tile = held.tile([P, S // 16], U16, name=name)
            nc.sync.dma_start(out=tile[:], in_=src)
            return tile

        pages = {}

        def load_page(i):
            if i in LATE_PAGE_TAGS:
                pages[i] = rotate(LATE_PAGE_TAGS[i], 1, [P, T2], F32)
            else:
                pages[i] = rotate("page", PAGES, [P, T2], F32)
            nc.sync.dma_start(out=pages[i][:], in_=page_rows[i // PACK, i % PACK])

        wgs_rows = wgs.rearrange("(p t) s -> p t s", t=PACK)
        wgs_first = keep("wgs_first", [P, S], F32)
        wgs_rest = keep("wgs_rest", [P, PACK - 1, S], F32)

        load_w1(0, 0)
        list1 = load_list("list1", offs)
        load_tab(0)
        load_w1(1, 0)
        for q in (0, 2, 1, 3):
            nc.sync.dma_start(out=wgs_first[32 * q : 32 * q + 32, :], in_=wgs_rows[:, 0, :])
        load_tab(1)
        list2 = load_list("list2", offs2)
        load_page(0)
        list3 = load_list("list3", offs3)
        for q in (0, 2, 1, 3):
            nc.sync.dma_start(out=wgs_rest[32 * q : 32 * q + 32, :, :], in_=wgs_rows[:, 1:PACK, :])
        load_page(1)
        load_w1(0, 1)
        load_w1(1, 1)
        w5_raw = {}
        w4_w = keep("w4_w", [P, 2, 2 * N], U8)

        def load_w5():
            for b in range(2):
                w5_raw[b] = rotate(f"xs{b}", 1, [P, PACK, N], F32)
                rows = w5[GROUP * b : GROUP * (b + 1), :]
                nc.sync.dma_start(out=w5_raw[b][:], in_=rows.rearrange("(p j) c -> p j c", j=PACK))

        def load_w4():
            nc.sync.dma_start(out=w4_w[:].bitcast(I32), in_=w4_words.rearrange("a p c -> p a c").bitcast(I32))
            for q in range(4):
                nc.sync.dma_start(
                    out=w4_s[32 * q : 32 * q + 4, :, :].bitcast(I32),
                    in_=w4_scales[:, 4 * q : 4 * q + 4, :].rearrange("a r n -> r a n").bitcast(I32),
                )

        def copy_on(engine, out, in_):
            if engine == "vector":
                nc.vector.tensor_copy(out=out, in_=in_)
            else:
                nc.scalar.copy(out=out, in_=in_)

        def interleave(planes, width, engine="scalar", grouped=None):
            if grouped is None:
                grouped = rotate("bf", 4, [P, PACK * width], BF16)
            if engine == "vector":
                nc.vector.tensor_copy(
                    out=grouped[:].rearrange("p (c t) -> p c t", t=PACK), in_=planes.rearrange("p t c -> p c t")
                )
            else:
                nc.scalar.copy(
                    out=grouped[:].rearrange("p (c i t) -> p c t i", i=4, t=PACK),
                    in_=planes.rearrange("p t (c i) -> p c t i", i=4),
                )
            return grouped

        def quantize(grouped, codes, scales):
            nc.vector.quantize_mx(out=codes.bitcast(FP8X4), scales=scales, in_=grouped[:])

        w1_c, w1_s = {}, {}
        w1_all = rotate("w1_c", 1, [P, 4 * GROUP], U32)

        def prepare_w1(a, b, engine="scalar"):
            grouped = rotate("bf", 4, [P, PACK * GROUP], BF16)
            copy_on(
                engine,
                grouped[:].rearrange("p (t m j) -> p m j t", t=PACK, j=PACK),
                w1_raw[a, b][:].rearrange("p j (m t) -> p m j t", t=PACK),
            )
            w1_c[a, b] = w1_all[:, GROUP * (2 * b + a) : GROUP * (2 * b + a + 1)]
            w1_s[a, b] = keep(f"w1_s{a}{b}", [P, GROUP], U8)
            quantize(grouped, w1_c[a, b][:], w1_s[a, b][:])

        w5_c = keep("w5_c", [P, 2, N], U32)
        w5_s = keep("w5_s", [P, 2, N], U8)

        def prepare_w5(b):
            quantize(interleave(w5_raw[b][:], N), w5_c[:, b, :], w5_s[:, b, :])

        v_both = rotate("v_w", 1, [P, 2 * S], U32)
        v_w = [v_both[:, S * a : S * (a + 1)] for a in range(2)]
        v_s = keep("v_s", [P, S], U8)

        def cols(jh):
            return slice(HALF * jh, HALF * (jh + 1))

        def entries(offsets, jh):
            return offsets[:, LIST_COLS * jh : LIST_COLS * (jh + 1)]

        h4, xs, picked, wide = {}, {}, {}, {}
        h_c, h_s, x_c, x_s = {}, {}, {}, {}

        def make_h(i, halves=(0, 1), pieces=1, between=None):
            b, t = divmod(i, PACK)
            work = []
            for jh in halves:
                acc = psum.tile([P, HALF], F32, name="bank", tag="bank")
                for a in range(2):
                    nc.tensor.matmul_mx(
                        out=acc[:],
                        lhsT=w1_c[a, b][:, P * t : P * (t + 1)].bitcast(FP8X4),
                        lhsT_scale=w1_s[a, b][:, P * t : P * (t + 1)],
                        rhs=v_w[a][:, cols(jh)].bitcast(FP8X4),
                        rhs_scale=v_s[4 * a : P, cols(jh)],
                        start=(a == 0),
                        stop=(a == 1),
                    )
                tmp = rotate("tmp", 3, [P, HALF], F32)
                if t == 0:
                    h4[b, jh] = rotate("h4", 3, [P, PACK, HALF], F32)
                for c0 in range(0, HALF, HALF // pieces):
                    part = slice(c0, c0 + HALF // pieces)
                    nc.scalar.activation(out=tmp[:, part], in_=acc[:, part], func=ACT.Tanh, bias=zero[:])
                    work.append((tmp[:, part], h4[b, jh][:, t, part]))
            for tmp, dest in work:
                nc.scalar.activation(out=tmp, in_=tmp, func=ACT.Sin, scale=half_depth[:, b, t : t + 1])
            for tmp, dest in work:
                nc.scalar.activation(out=tmp, in_=tmp, func=ACT.Square)
            for k, (tmp, dest) in enumerate(work):
                nc.scalar.activation(
                    out=dest, in_=tmp, func=ACT.Identity,
                    scale=neg2_gain[:, b, t : t + 1], bias=vec["gain"][:, b, t : t + 1],
                )
                if k == 0 and between is not None:
                    scale_x(between)

        def put(i, jh):
            b, t = divmod(i, PACK)
            weights = wgs_first[:] if t == 0 else wgs_rest[:, t - 1, :]
            nc.vector.tensor_tensor(
                pages[i][:].indirect(entries(list2, jh)), h4[b, jh][:, t, :], weights[:, cols(jh)], ALU.mult
            )

        def pick(i, halves=False):
            picked[i] = rotate("picked", 2, [P, NP], F32)
            if halves:
                for jh in range(2):
                    nc.vector.tensor_copy(out=picked[i][:, cols(jh)], in_=pages[i][:].indirect(entries(list3, jh)))
            else:
                nc.vector.tensor_copy(out=picked[i][:], in_=pages[i][:].indirect(list3[:]))

        def change_page(i):
            put(i, 0)
            if i > 0:
                pick(i - 1)
            put(i, 1)
            spread(i, 0)
            spread(i, 1)

        def spread(i, ch):
            b, t = divmod(i, PACK)
            if t == 0:
                wide[b, ch] = rotate(f"wide{ch}", 1, [P, PACK, WIDE], F32)
            nc.sync.dma_start(out=wide[b, ch][:, t, :], in_=pages[i][:, WIDE * ch : WIDE * (ch + 1)])

        def store_page(i):
            queue = nc.gpsimd if PACK <= i < 2 * PACK - 1 else nc.sync
            queue.dma_start(out=out_rows[i // PACK, i % PACK], in_=pages[i][:])

        def scale_x(i, part=slice(0, NP)):
            b, t = divmod(i, PACK)
            if t == 0:
                xs[b] = rotate(f"xs{b}", 1, [P, PACK, NP], BF16)
            nc.scalar.activation(
                out=xs[b][:, t, part], in_=picked[i][:, part], func=ACT.Copy, scale=vec["sc"][:, b, t : t + 1]
            )

        def quantize_h(b):
            for jh in range(2):
                h_c[b, jh] = keep(f"h_c{b}{jh}", [P, HALF], U32)
                h_s[b, jh] = keep(f"h_s{b}{jh}", [P, HALF], U8)
                quantize(interleave(h4[b, jh][:], HALF), h_c[b, jh][:], h_s[b, jh][:])

        def quantize_x(b, jh, engine="scalar"):
            x_c[b, jh] = keep(f"x_c{b}{jh}", [P, HALF], U32)
            x_s[b, jh] = keep(f"x_s{b}{jh}", [P, HALF], U8)
            quantize(interleave(xs[b][:, :, cols(jh)], HALF, engine), x_c[b, jh][:], x_s[b, jh][:])

        plane_s = keep("plane_s", [P, T2], U8)

        def quantize_page(b, ch, engines):
            queue = nc.gpsimd if b == 0 else nc.sync
            codes = rotate("plane_c", 2, [P, WIDE], U32)
            words = out_2[b].rearrange("p m t -> p (m t)").bitcast(I32)
            if (b, ch) == (1, 1):
                both = rotate("xs1", 1, [P, PACK * WIDE], BF16)
            else:
                both = rotate("raw", 2, [P, PACK * WIDE], BF16)
            for u in range(2):
                part = both[:, PACK * HALF * u : PACK * HALF * (u + 1)]
                grouped = interleave(wide[b, ch][:, :, cols(u)], HALF, engines[u], part)
                c0 = WIDE * ch + HALF * u
                quantize(grouped, codes[:, cols(u)], plane_s[4 * b : P, c0 : c0 + HALF])
            queue.dma_start(out=words[:, WIDE * ch : WIDE * (ch + 1)], in_=codes[:].bitcast(I32))
            if ch == 1:
                for q in range(4):
                    queue.dma_start(
                        out=out_3[b, 4 * q : 4 * q + 4, :].bitcast(I32),
                        in_=plane_s[32 * q + 4 * b : 32 * q + 4 * b + 4, :].bitcast(I32),
                    )

        sums = {}

        def second_pass(kind, b, jh):
            for n in range(N_TILES):
                first = kind == "h" and b == 0
                last = kind == "x" and b == 1
                if first:
                    sums[n, jh] = psum.tile([P, HALF], F32, name="bank", tag="bank")
                if kind == "h":
                    lhs = w5_c[:, b, P * n : P * (n + 1)].bitcast(FP8X4)
                    lhs_s = w5_s[:, b, P * n : P * (n + 1)]
                    rhs, rhs_s = h_c[b, jh], h_s[b, jh]
                else:
                    lhs = w4_w[:, b, 2 * P * n : 2 * P * (n + 1)].bitcast(FP4X4)
                    lhs_s = w4_s[:, b, P * n : P * (n + 1)]
                    rhs, rhs_s = x_c[b, jh], x_s[b, jh]
                nc.tensor.matmul_mx(
                    out=sums[n, jh][:], lhsT=lhs, lhsT_scale=lhs_s,
                    rhs=rhs[:].bitcast(FP8X4), rhs_scale=rhs_s[:], start=first, stop=last,
                )

        def store_y():
            result = rotate("wide0", 1, [P, 2 * N_TILES * HALF], F32)
            for jh in range(2):
                for n in range(N_TILES):
                    part = result[:, cols(N_TILES * jh + n)]
                    nc.scalar.copy(out=part, in_=sums[n, jh][:])
                written = result[:, N_TILES * HALF * jh : N_TILES * HALF * (jh + 1)]
                nc.scalar.dma_start(
                    out=out_0[:, cols(jh)].rearrange("(n p) c -> p n c", p=P),
                    in_=written.rearrange("p (n c) -> p n c", n=N_TILES),
                )

        prepare_w1(0, 0)
        nc.vector.tensor_copy(out=v_w[0][:], in_=tab_w[0][:].indirect(list1[:]))
        nc.vector.tensor_copy(out=v_s[:], in_=tab_s[:].indirect(list1[:]))
        prepare_w1(1, 0)
        for jh in range(2):
            nc.vector.tensor_copy(out=v_w[1][:, cols(jh)], in_=tab_w[1][:].indirect(entries(list1, jh)))

        load_page(2)
        load_w5()
        load_page(3)
        load_page(4)
        make_h(0, (0,), 2)
        make_h(0, (1,), 2)
        change_page(0)
        make_h(1)
        change_page(1)
        prepare_w1(0, 1)
        prepare_w1(1, 1)
        make_h(2)
        change_page(2)
        prepare_w5(0)
        prepare_w5(1)
        load_page(5)
        make_h(3, between=0)
        change_page(3)
        load_page(6)
        load_page(7)
        load_w4()
        quantize_h(0)
        make_h(4, between=1)
        change_page(4)
        make_h(5, between=2)
        change_page(5)
        quantize_page(0, 0, ("scalar", "scalar"))
        store_page(0)
        store_page(1)
        store_page(2)
        make_h(6, between=3)
        change_page(6)
        quantize_page(0, 1, ("scalar", "scalar"))
        store_page(3)
        store_page(4)
        store_page(5)
        make_h(7, between=4)
        store_page(6)
        change_page(7)
        quantize_x(0, 0)
        quantize_x(0, 1)
        scale_x(5)
        quantize_h(1)
        pick(7, halves=True)
        store_page(7)
        scale_x(6)
        for kind, b in (("h", 0), ("x", 0), ("h", 1)):
            for jh in range(2):
                second_pass(kind, b, jh)
        for jh in range(2):
            scale_x(7, cols(jh))
            quantize_x(1, jh, ("scalar", "vector")[jh])
            second_pass("x", 1, jh)
        quantize_page(1, 0, ("scalar", "scalar"))
        quantize_page(1, 1, ("vector", "vector"))
        store_y()
